import numpy as np
import ml_dtypes


def mxq(x, axis, fmt="e4m3"):
    dtype, down = {"e4m3": (ml_dtypes.float8_e4m3fn, 7), "e5m2": (ml_dtypes.float8_e5m2, 14)}[fmt]
    v = np.moveaxis(np.asarray(x, np.float32).astype(ml_dtypes.bfloat16).astype(np.float64), axis, -1)
    blocks = v.reshape(v.shape[:-1] + (-1, 32))
    amax = np.abs(blocks).max(-1, keepdims=True)
    byte = np.maximum(np.where(amax > 0, np.frexp(amax)[1] - 1 + 127, 0) - down, 1)
    scale = np.exp2(byte - 127.0)
    codes = (blocks / scale).astype(np.float32).astype(dtype).astype(np.float64)
    return np.moveaxis((codes * scale).reshape(v.shape), -1, axis)


WIDE = False


def mx_kscale(k):
    if not WIDE:
        return np.ones(k)
    levels = np.array([10, -10, 5, -5, 0])
    if k % 512:
        return np.exp2(np.random.permutation(np.resize(levels, k // 32))).repeat(32)
    a = np.empty((k // 512, 16))
    for p in range(k // 512):
        a[p, :8] = np.random.permutation(np.resize(levels, 8))
        for g in range(8):
            far = levels[np.abs(levels - a[p, g]) >= 10]
            a[p, g + 8] = far[np.random.randint(len(far))]
    return np.exp2(a.ravel()).repeat(32)


def f64(x):
    return np.asarray(x).astype(np.float64)


def striped(idx):
    return np.tile(idx.reshape(-1, 16).T, (8, 1)).astype(np.uint16)


def unstriped(offs):
    return offs[:16].T.reshape(-1).astype(np.int64)


def pack_weight(w):
    k, n = w.shape
    w = f64(np.asarray(w, np.float32).astype(ml_dtypes.bfloat16)).reshape(k // 32, 32, n)
    amax = np.abs(w).max(1)
    byte = np.clip(np.where(amax > 0, np.frexp(amax)[1] - 1 + 127 - 7, 1), 1, 254)
    scaled = (w * np.exp2(127.0 - byte)[:, None, :]).reshape(k, n).astype(np.float32)
    words = np.ascontiguousarray(scaled.reshape(k // 512, 128, 4, n).transpose(0, 1, 3, 2)).astype(ml_dtypes.float8_e4m3fn).view(np.uint8)
    return words, np.ascontiguousarray(byte.astype(np.uint8).reshape(k // 512, 16, n))


def unpack_weight(words, scales):
    g, p, n, _ = words.shape
    vals = np.ascontiguousarray(words).view(ml_dtypes.float8_e4m3fn).astype(np.float64) * np.repeat(np.exp2(scales.astype(np.float64) - 127.0), 8, axis=1)[..., None]
    return vals.transpose(0, 1, 3, 2).reshape(g * 512, n)


def sigmoid(v):
    return 1.0 / (1.0 + np.exp(-np.maximum(v, -700.0)))


def gelu(v):
    return 0.5 * v * (1.0 + np.tanh(np.sqrt(2.0 / np.pi) * (v + 0.044715 * v**3)))


K, T, S, H, Z, W = 512, 2048, 512, 512, 512, 2048
P = 2 ** 7


def setup_inputs():
    n = np.random.standard_normal
    s = mx_kscale(K)[:, None]
    u = mx_kscale(H)
    packed_xT = pack_weight(n((K, T)) * s)
    packed_eT = pack_weight(n((K, W)) * s)
    return {
        "x_words": packed_xT[0],
        "x_scales": packed_xT[1],
        "w1": (n((K, H)) / np.sqrt(K) / s).astype(np.float32),
        "e_words": packed_eT[0],
        "e_scales": packed_eT[1],
        "w2": (n((K, H)) / np.sqrt(K) / s).astype(np.float32),
        "w3": (n((K, H)) / np.sqrt(K) / s).astype(np.float32),
        "unit": (np.random.uniform(0.6, 1.4, (H, 1)) * u[:, None]).astype(np.float32),
        "unit2": (np.random.uniform(0.6, 1.4, (H, 1)) / np.sqrt(H) / u[:, None]).astype(np.float32),
        "abd": (np.tile(np.random.uniform(0.2, 1.5, W), (P, 1))).astype(np.float32),
        "offs": striped(np.random.permutation(T)[:S]),
        "pry": striped(np.random.permutation(W)[:Z]),
        "ref": striped(np.random.permutation(Z)),
        "sw": striped(np.random.permutation(Z)),
    }


def reference(x_words, x_scales, w1, e_words, e_scales, w2, w3, unit, unit2, abd, offs, pry, ref, sw):
    xq = unpack_weight(x_words, x_scales)[:, unstriped(offs)]
    y = mxq(f64(w1), 0, "e4m3").T @ xq
    att = gelu(y)
    hid = f64(unit) * att
    e_pry = unpack_weight(e_words, e_scales)[:, unstriped(pry)]
    ye = mxq(f64(w2), 0, "e4m3").T @ e_pry
    yg = mxq(f64(w3), 0, "e4m3").T @ e_pry
    gr = yg[:, unstriped(ref)]
    vul = ye * (-0.7 * sigmoid(gr) + 1.2)
    hid2 = f64(unit2) * vul
    sc = mxq(hid, 0, "e4m3").T @ mxq(hid2, 0, "e4m3")
    rate = (np.exp(1.2 * np.tanh(sc))) * (f64(abd)[:1][:, unstriped(pry)])
    tot = rate.mean(axis=1, keepdims=True)
    feed = rate / (tot + 0.5)
    return feed - (0.5 * feed[:, unstriped(sw)])

@@ -1,0 +1,235 @@
+from contextlib import ExitStack
+
+import concourse.mybir as mybir
+
+F32 = mybir.dt.float32
+BF16 = mybir.dt.bfloat16
+I32 = mybir.dt.int32
+U32 = mybir.dt.uint32
+U16 = mybir.dt.uint16
+U8 = mybir.dt.uint8
+FP8X4 = mybir.dt.float8_e4m3fn_x4
+ACT = mybir.ActivationFunctionType
+ALU = mybir.AluOpType
+
+P = 128
+PACK = 4
+K = 512
+N = 512
+TABLE = 2048
+HALF = N // 2
+BLOCKS = N // P
+FLOPS = 4 * 2 * K * N * N
+
+
+def tile_picked_yfoodwb_sw_p_kernel(
+    tc, x_words, x_scales, w1, e_words, e_scales, w2, w3, unit, unit2, abd, offs, pry, ref, sw, out
+):
+    nc = tc.nc
+    with ExitStack() as ctx:
+        keep = ctx.enter_context(tc.tile_pool(name="keep", bufs=1))
+        ring = ctx.enter_context(tc.tile_pool(name="ring", bufs=2))
+        psum = ctx.enter_context(tc.psum_pool(name="psum", bufs=1))
+
+        def load_list(src, name):
+            t = keep.tile([P, N // 16], U16, name=name)
+            nc.sync.dma_start(t[:], src)
+            return t
+
+        def load_weight(src, name, tag):
+            t = keep.tile([P, PACK, N], F32, name=name, tag=tag, align_bytes=64)
+            nc.sync.dma_start(out=t[:], in_=src.rearrange("(p j) c -> p j c", j=PACK))
+            return t
+
+        def load_words(src, name, tag):
+            t = keep.tile([P, TABLE], I32, name=name, tag=tag, align_bytes=64)
+            nc.sync.dma_start(out=t[:], in_=src[0].rearrange("p c r -> p (c r)").bitcast(I32))
+            return t
+
+        def load_scale_bytes(src, name, first_row, clear, queue):
+            t = keep.tile([P, TABLE], U8, name=name, align_bytes=64)
+            clear.memset(t[:].bitcast(I32), 0)
+            for q in range(4):
+                queue.dma_start(
+                    out=t[32 * q + first_row : 32 * q + first_row + 4, :].bitcast(I32),
+                    in_=src[0, 4 * q : 4 * q + 4, :].bitcast(I32),
+                )
+            return t
+
+        def load_rows_factor(src, name):
+            t = keep.tile([P, PACK], F32, name=name)
+            nc.gpsimd.dma_start(out=t[:], in_=src.rearrange("(p t) o -> p (t o)", t=PACK))
+            return t
+
+        def gather(table, idx, dtype, name):
+            t = keep.tile([P, N], dtype, name=name, align_bytes=64)
+            nc.vector.tensor_copy(t[:], table.indirect(idx[:]))
+            return t
+
+        def round_weight(raw, name, scalar_share=0):
+            g = keep.tile([P, PACK, P, PACK], BF16, name=name, align_bytes=64)
+            dst = g[:].rearrange("p t m j -> p m j t")
+            src = raw[:].rearrange("p j (m t) -> p m j t", t=PACK)
+            if scalar_share:
+                nc.scalar.copy(out=dst[:, :scalar_share], in_=src[:, :scalar_share])
+            nc.vector.tensor_copy(out=dst[:, scalar_share:], in_=src[:, scalar_share:])
+            return g
+
+        def quantize_weight(g, name):
+            codes = keep.tile([P, N], U32, name=name + "_codes", align_bytes=64)
+            scales = keep.tile([P, N], U8, name=name + "_scales", align_bytes=64)
+            nc.vector.quantize_mx(
+                out=codes[:].bitcast(FP8X4), scales=scales[:], in_=g[:].rearrange("p t m j -> p (t m j)")
+            )
+            return codes, scales
+
+        def product(acc, lhs, lhs_cols, rhs, rhs_cols):
+            nc.tensor.matmul_mx(
+                out=acc,
+                lhsT=lhs[0][:, lhs_cols].bitcast(FP8X4),
+                lhsT_scale=lhs[1][:, lhs_cols],
+                rhs=rhs[0][:, rhs_cols].bitcast(FP8X4),
+                rhs_scale=rhs[1][:, rhs_cols],
+                start=True,
+                stop=True,
+            )
+
+        def cols(b, width=P):
+            return slice(b * width, (b + 1) * width)
+
+        E_ROW = 4
+        pry_t = load_list(pry, "pry_t")
+        w3_raw = load_weight(w3, "w3_raw", "w3_raw")
+        e_scale_table = load_scale_bytes(e_scales, "e_scale_table", E_ROW, nc.vector, nc.sync)
+        e_table = load_words(e_words, "e_table", "e_table")
+        offs_t = load_list(offs, "offs_t")
+        x_scale_table = load_scale_bytes(x_scales, "x_scale_table", 0, nc.vector, nc.sync)
+        w2_raw = load_weight(w2, "w2_raw", "w2_raw")
+        ref_t = load_list(ref, "ref_t")
+        w1_raw = load_weight(w1, "w1_raw", "w1_raw")
+        x_table = load_words(x_words, "x_table", "x_table")
+        sw_t = load_list(sw, "sw_t")
+        abd_t = keep.tile([P, TABLE], F32, name="abd_t")
+        nc.sync.dma_start(out=abd_t[:], in_=abd)
+        unit2_t = load_rows_factor(unit2, "unit2_t")
+        unit_t = load_rows_factor(unit, "unit_t")
+
+        slope = keep.tile([P, PACK], F32, name="slope")
+        level = keep.tile([P, PACK], F32, name="level")
+        nc.gpsimd.tensor_scalar(slope[:], unit2_t[:], -0.35, 0.0, ALU.mult, ALU.add)
+        nc.gpsimd.tensor_scalar(level[:], unit2_t[:], 0.85, 0.0, ALU.mult, ALU.add)
+
+        e_picked_scales = gather(e_scale_table[:], pry_t, U8, "e_picked_scales")
+        w3q = quantize_weight(round_weight(w3_raw, "w3_bf", 48), "w3")
+        e_picked_words = gather(e_table[:].bitcast(U32), pry_t, U32, "e_picked_words")
+        e_picked = (e_picked_words, e_picked_scales[E_ROW:P, :])
+        x_picked_scales = gather(x_scale_table[:], offs_t, U8, "x_picked_scales")
+
+        refuge = []
+        for t in range(PACK):
+            yg = psum.tile([P, N], F32, name="yg", tag="a%d" % t)
+            product(yg[:], w3q, cols(t), e_picked, slice(0, N))
+            f = keep.tile([P, N], F32, name="refuge%d" % t)
+            nc.scalar.activation(f[:], yg[:], ACT.Tanh, scale=0.5)
+            refuge.append(f)
+        w2_bf = round_weight(w2_raw, "w2_bf")
+        factor = keep.tile([P, PACK, N], F32, name="factor", tag="w2_raw", align_bytes=64)
+        for t in range(PACK):
+            nc.vector.tensor_scalar(
+                factor[:, t, :], refuge[t][:], slope[:, t : t + 1], level[:, t : t + 1], ALU.mult, ALU.add
+            )
+        w2q = quantize_weight(w2_bf, "w2")
+
+        fetched = [keep.tile([P, PACK, HALF], F32, name="fetched%d" % h) for h in range(2)]
+        for h in range(2):
+            for t in range(PACK):
+                nc.scalar.activation(fetched[h][:, t, :], factor[:, t, :].indirect(ref_t[:, cols(h, 16)]), ACT.Copy)
+
+        ye = []
+        for b in range(BLOCKS):
+            bank = psum.tile([P, PACK, P], F32, name="ye", tag="b%d" % b)
+            for t in range(PACK):
+                product(bank[:, t, :], w2q, cols(t), e_picked, cols(b))
+            ye.append(bank)
+
+        w1q = quantize_weight(round_weight(w1_raw, "w1_bf"), "w1")
+        x_picked_words = gather(x_table[:].bitcast(U32), offs_t, U32, "x_picked_words")
+        x_picked = (x_picked_words, x_picked_scales)
+
+        att = []
+        for b in range(BLOCKS):
+            bank = psum.tile([P, PACK, P], F32, name="y", tag="a%d" % b)
+            for t in range(PACK):
+                product(bank[:, t, :], w1q, cols(t), x_picked, cols(b))
+            a = keep.tile([P, P, PACK], F32, name="att%d" % b)
+            nc.scalar.activation(a[:], bank[:].rearrange("p t j -> p j t"), ACT.Gelu_apprx_tanh)
+            att.append(a)
+
+        hid2_bf = keep.tile([P, N, PACK], BF16, name="hid2_bf", tag="x_table", align_bytes=64)
+        for b in range(BLOCKS):
+            nc.vector.tensor_tensor(
+                hid2_bf[:, cols(b), :].rearrange("p (c i) t -> p c t i", i=4),
+                ye[b][:].rearrange("p t (c i) -> p c t i", i=4),
+                fetched[b // 2][:, :, cols(b % 2)].rearrange("p t (c i) -> p c t i", i=4),
+                ALU.mult,
+            )
+        hid2_codes = keep.tile([P, N], U32, name="hid2_codes", align_bytes=64)
+        hid2_scales = keep.tile([P, N], U8, name="hid2_scales", align_bytes=64)
+        for h in range(2):
+            nc.vector.quantize_mx(
+                out=hid2_codes[:, cols(h, HALF)].bitcast(FP8X4),
+                scales=hid2_scales[:, cols(h, HALF)],
+                in_=hid2_bf[:, cols(h, HALF), :].rearrange("p e t -> p (e t)"),
+            )
+
+
+        def scores(b):
+            hid_bf = keep.tile([P, P, PACK], BF16, name="hid_bf%d" % b, align_bytes=64)
+            nc.vector.tensor_tensor(
+                hid_bf[:], att[b][:], unit_t[:].unsqueeze(1).to_broadcast([P, P, PACK]), ALU.mult
+            )
+            codes = keep.tile([P, P], U32, name="hid_codes%d" % b, align_bytes=64)
+            scales = keep.tile([P, P], U8, name="hid_scales%d" % b, align_bytes=64)
+            nc.vector.quantize_mx(
+                out=codes[:].bitcast(FP8X4), scales=scales[:], in_=hid_bf[:].rearrange("p j t -> p (j t)")
+            )
+            sc = psum.tile([P, N], F32, name="sc", tag="b%d" % b)
+            product(sc[:], (codes, scales), slice(0, P), (hid2_codes, hid2_scales), slice(0, N))
+            return sc
+
+        def grow(b, sc):
+            bounded = ring.tile([P, N], F32, name="bounded")
+            nc.scalar.activation(bounded[:], sc[:], ACT.Tanh)
+            grown = keep.tile([P, N], F32, name="grown%d" % b)
+            nc.scalar.activation(grown[:], bounded[:], ACT.Exp, scale=1.2)
+            return grown
+
+        def finish(b, grown):
+            rate = keep.tile([P, N], F32, name="rate%d" % b)
+            total = keep.tile([P, 1], F32, name="total%d" % b)
+            nc.vector.scalar_tensor_tensor(
+                rate[:], grown[:], 1.0, abd_picked[:], ALU.mult, ALU.mult, accum_out=total[:]
+            )
+            denom = keep.tile([P, 1], F32, name="denom%d" % b)
+            nc.vector.tensor_scalar(denom[:], total[:], 1.0 / N, 0.5, ALU.mult, ALU.add)
+            inv = keep.tile([P, 1], F32, name="inv%d" % b)
+            nc.vector.reciprocal(inv[:], denom[:])
+            other = keep.tile([P, N], F32, name="other%d" % b)
+            nc.vector.tensor_scalar(other[:], rate[:], inv[:], -0.5, ALU.mult, ALU.mult)
+            lo, hi = cols(0, HALF), cols(1, HALF)
+            feed_lo = keep.tile([P, HALF], F32, name="feed_lo%d" % b)
+            nc.scalar.activation(feed_lo[:], rate[:, lo], ACT.Copy, scale=inv[:])
+            other_hi = keep.tile([P, HALF], F32, name="other_hi%d" % b)
+            nc.scalar.activation(other_hi[:], other[:].indirect(sw_t[:, cols(1, 16)]), ACT.Copy)
+            res = keep.tile([P, N], F32, name="res%d" % b)
+            nc.vector.tensor_tensor(res[:, lo], other[:].indirect(sw_t[:, cols(0, 16)]), feed_lo[:], ALU.add)
+            nc.vector.scalar_tensor_tensor(res[:, hi], rate[:, hi], inv[:], other_hi[:], ALU.mult, ALU.add)
+            nc.sync.dma_start(out=out[cols(b), :], in_=res[:])
+
+        sc = [scores(b) for b in range(BLOCKS)]
+        abd_picked = gather(abd_t[:], pry_t, F32, "abd_picked")
+        grown = grow(0, sc[0])
+        for b in range(BLOCKS):
+            ahead = grow(b + 1, sc[b + 1]) if b + 1 < BLOCKS else None
+            finish(b, grown)
+            grown = ahead

@@ -47,7 +47,7 @@ def tile_picked_yfoodwb_sw_p_kernel(
             return t
 
         def load_scale_bytes(src, name, first_row, clear, queue):
-            t = keep.tile([P, TABLE], U8, name=name, align_bytes=64)
+            t = keep.tile([P, TABLE], U8, name=name, tag=name, align_bytes=64)
             clear.memset(t[:].bitcast(I32), 0)
             for q in range(4):
                 queue.dma_start(
@@ -66,6 +66,12 @@ def tile_picked_yfoodwb_sw_p_kernel(
             nc.vector.tensor_copy(t[:], table.indirect(idx[:]))
             return t
 
+        def gather_words(table, idx, name):
+            t = keep.tile([P, N], U32, name=name, align_bytes=64)
+            for h in range(2):
+                nc.vector.tensor_copy(t[:, cols(h, HALF)], table[:].bitcast(U32).indirect(idx[:, cols(h, 16)]))
+            return t
+
         def round_weight(raw, name, scalar_share=0):
             g = keep.tile([P, PACK, P, PACK], BF16, name=name, align_bytes=64)
             dst = g[:].rearrange("p t m j -> p m j t")
@@ -75,8 +81,8 @@ def tile_picked_yfoodwb_sw_p_kernel(
             nc.vector.tensor_copy(out=dst[:, scalar_share:], in_=src[:, scalar_share:])
             return g
 
-        def quantize_weight(g, name):
-            codes = keep.tile([P, N], U32, name=name + "_codes", align_bytes=64)
+        def quantize_weight(g, name, tag=None):
+            codes = keep.tile([P, N], U32, name=name + "_codes", tag=tag or name, align_bytes=64)
             scales = keep.tile([P, N], U8, name=name + "_scales", align_bytes=64)
             nc.vector.quantize_mx(
                 out=codes[:].bitcast(FP8X4), scales=scales[:], in_=g[:].rearrange("p t m j -> p (t m j)")
@@ -98,8 +104,12 @@ def tile_picked_yfoodwb_sw_p_kernel(
             return slice(b * width, (b + 1) * width)
 
         E_ROW = 4
-        pry_t = load_list(pry, "pry_t")
+        warm = keep.tile([P, 1], F32, name="warm")
+        nc.gpsimd.memset(warm[:], 0.0)
+        warm_gelu = keep.tile([P, 1], F32, name="warm_gelu")
+        nc.scalar.activation(warm_gelu[:], warm[:], ACT.Gelu_apprx_tanh)
         w3_raw = load_weight(w3, "w3_raw", "w3_raw")
+        pry_t = load_list(pry, "pry_t")
         e_scale_table = load_scale_bytes(e_scales, "e_scale_table", E_ROW, nc.vector, nc.sync)
         e_table = load_words(e_words, "e_table", "e_table")
         offs_t = load_list(offs, "offs_t")
@@ -114,36 +124,30 @@ def tile_picked_yfoodwb_sw_p_kernel(
         unit2_t = load_rows_factor(unit2, "unit2_t")
         unit_t = load_rows_factor(unit, "unit_t")
 
-        slope = keep.tile([P, PACK], F32, name="slope")
-        level = keep.tile([P, PACK], F32, name="level")
-        nc.gpsimd.tensor_scalar(slope[:], unit2_t[:], -0.35, 0.0, ALU.mult, ALU.add)
-        nc.gpsimd.tensor_scalar(level[:], unit2_t[:], 0.85, 0.0, ALU.mult, ALU.add)
-
         e_picked_scales = gather(e_scale_table[:], pry_t, U8, "e_picked_scales")
-        w3q = quantize_weight(round_weight(w3_raw, "w3_bf", 48), "w3")
-        e_picked_words = gather(e_table[:].bitcast(U32), pry_t, U32, "e_picked_words")
+        w3q = quantize_weight(round_weight(w3_raw, "w3_bf", 80), "w3", "e_scale_table")
+        e_picked_words = gather_words(e_table, pry_t, "e_picked_words")
         e_picked = (e_picked_words, e_picked_scales[E_ROW:P, :])
         x_picked_scales = gather(x_scale_table[:], offs_t, U8, "x_picked_scales")
 
-        refuge = []
-        for t in range(PACK):
-            yg = psum.tile([P, N], F32, name="yg", tag="a%d" % t)
-            product(yg[:], w3q, cols(t), e_picked, slice(0, N))
-            f = keep.tile([P, N], F32, name="refuge%d" % t)
-            nc.scalar.activation(f[:], yg[:], ACT.Tanh, scale=0.5)
-            refuge.append(f)
+        refuge = keep.tile([P, PACK, N], F32, name="refuge")
+        for h in range(2):
+            for u in range(2):
+                yg = psum.tile([P, 2, HALF], F32, name="yg", tag="a%d" % (2 * h + u))
+                for s in range(2):
+                    product(yg[:, s, :], w3q, cols(2 * u + s), e_picked, cols(h, HALF))
+                nc.scalar.activation(refuge[:, cols(u, 2), cols(h, HALF)], yg[:], ACT.Tanh, scale=0.5)
         w2_bf = round_weight(w2_raw, "w2_bf")
-        factor = keep.tile([P, PACK, N], F32, name="factor", tag="w2_raw", align_bytes=64)
-        for t in range(PACK):
-            nc.vector.tensor_scalar(
-                factor[:, t, :], refuge[t][:], slope[:, t : t + 1], level[:, t : t + 1], ALU.mult, ALU.add
-            )
         w2q = quantize_weight(w2_bf, "w2")
 
         fetched = [keep.tile([P, PACK, HALF], F32, name="fetched%d" % h) for h in range(2)]
         for h in range(2):
             for t in range(PACK):
-                nc.scalar.activation(fetched[h][:, t, :], factor[:, t, :].indirect(ref_t[:, cols(h, 16)]), ACT.Copy)
+                piece = fetched[h][:, t, :]
+                nc.scalar.activation(
+                    piece, refuge[:, t, :].indirect(ref_t[:, cols(h, 16)]), ACT.Copy, scale=-0.35, bias=0.85
+                )
+                nc.gpsimd.tensor_scalar(piece, piece, unit2_t[:, t : t + 1], 0.0, ALU.mult, ALU.add)
 
         ye = []
         for b in range(BLOCKS):
@@ -153,7 +157,7 @@ def tile_picked_yfoodwb_sw_p_kernel(
             ye.append(bank)
 
         w1q = quantize_weight(round_weight(w1_raw, "w1_bf"), "w1")
-        x_picked_words = gather(x_table[:].bitcast(U32), offs_t, U32, "x_picked_words")
+        x_picked_words = gather_words(x_table, offs_t, "x_picked_words")
         x_picked = (x_picked_words, x_picked_scales)
 
         att = []
@@ -165,6 +169,12 @@ def tile_picked_yfoodwb_sw_p_kernel(
             nc.scalar.activation(a[:], bank[:].rearrange("p t j -> p j t"), ACT.Gelu_apprx_tanh)
             att.append(a)
 
+        WIDE = N + 1
+        abd_picked = keep.tile([P, WIDE], F32, name="abd_picked")
+        nc.gpsimd.memset(abd_picked[:, N:WIDE], N / 2.0)
+        nc.scalar.activation(abd_picked[:, :N], abd_t[:].indirect(pry_t[:]), ACT.Copy)
+        warm_exp = keep.tile([P, 1], F32, name="warm_exp")
+        nc.scalar.activation(warm_exp[:], att[BLOCKS - 1][:, 0, 0:1], ACT.Exp, scale=0.0)
         hid2_bf = keep.tile([P, N, PACK], BF16, name="hid2_bf", tag="x_table", align_bytes=64)
         for b in range(BLOCKS):
             nc.vector.tensor_tensor(
@@ -200,34 +210,41 @@ def tile_picked_yfoodwb_sw_p_kernel(
         def grow(b, sc):
             bounded = ring.tile([P, N], F32, name="bounded")
             nc.scalar.activation(bounded[:], sc[:], ACT.Tanh)
-            grown = keep.tile([P, N], F32, name="grown%d" % b)
-            nc.scalar.activation(grown[:], bounded[:], ACT.Exp, scale=1.2)
+            grown = keep.tile([P, WIDE], F32, name="grown%d" % b)
+            nc.gpsimd.memset(grown[:, N:WIDE], 1.0)
+            nc.scalar.activation(grown[:, :N], bounded[:], ACT.Exp, scale=1.2)
             return grown
 
         def finish(b, grown):
-            rate = keep.tile([P, N], F32, name="rate%d" % b)
+            rate = keep.tile([P, WIDE], F32, name="rate%d" % b)
             total = keep.tile([P, 1], F32, name="total%d" % b)
             nc.vector.scalar_tensor_tensor(
                 rate[:], grown[:], 1.0, abd_picked[:], ALU.mult, ALU.mult, accum_out=total[:]
             )
-            denom = keep.tile([P, 1], F32, name="denom%d" % b)
-            nc.vector.tensor_scalar(denom[:], total[:], 1.0 / N, 0.5, ALU.mult, ALU.add)
             inv = keep.tile([P, 1], F32, name="inv%d" % b)
-            nc.vector.reciprocal(inv[:], denom[:])
-            other = keep.tile([P, N], F32, name="other%d" % b)
-            nc.vector.tensor_scalar(other[:], rate[:], inv[:], -0.5, ALU.mult, ALU.mult)
-            lo, hi = cols(0, HALF), cols(1, HALF)
-            feed_lo = keep.tile([P, HALF], F32, name="feed_lo%d" % b)
-            nc.scalar.activation(feed_lo[:], rate[:, lo], ACT.Copy, scale=inv[:])
-            other_hi = keep.tile([P, HALF], F32, name="other_hi%d" % b)
-            nc.scalar.activation(other_hi[:], other[:].indirect(sw_t[:, cols(1, 16)]), ACT.Copy)
+            nc.vector.reciprocal(inv[:], total[:])
             res = keep.tile([P, N], F32, name="res%d" % b)
-            nc.vector.tensor_tensor(res[:, lo], other[:].indirect(sw_t[:, cols(0, 16)]), feed_lo[:], ALU.add)
-            nc.vector.scalar_tensor_tensor(res[:, hi], rate[:, hi], inv[:], other_hi[:], ALU.mult, ALU.add)
-            nc.sync.dma_start(out=out[cols(b), :], in_=res[:])
+            if b < BLOCKS - 2:
+                feed = keep.tile([P, WIDE], F32, name="feed%d" % b)
+                nc.vector.tensor_scalar(feed[:], rate[:], inv[:], float(N), ALU.mult, ALU.mult)
+                other = keep.tile([P, N], F32, name="other%d" % b)
+                nc.scalar.activation(other[:], feed[:].indirect(sw_t[:]), ACT.Copy, scale=-0.5)
+                nc.vector.tensor_tensor(res[:], feed[:, :N], other[:], ALU.add)
+                nc.sync.dma_start(out=out[cols(b), :], in_=res[:])
+                return
+            lo, hi = cols(0, HALF), cols(1, HALF)
+            neg = keep.tile([P, N], F32, name="neg%d" % b)
+            nc.vector.tensor_scalar(neg[:], rate[:, :N], inv[:], -0.5 * N, ALU.mult, ALU.mult)
+            feed_lo = keep.tile([P, HALF], F32, name="feed_lo%d" % b)
+            nc.vector.tensor_scalar(feed_lo[:], rate[:, lo], inv[:], float(N), ALU.mult, ALU.mult)
+            other_hi = keep.tile([P, HALF], F32, name="other_hi%d" % b)
+            nc.scalar.activation(other_hi[:], neg[:].indirect(sw_t[:, cols(1, 16)]), ACT.Copy)
+            nc.vector.tensor_tensor(res[:, lo], neg[:].indirect(sw_t[:, cols(0, 16)]), feed_lo[:], ALU.add)
+            nc.sync.dma_start(out=out[cols(b), lo], in_=res[:, lo])
+            nc.vector.scalar_tensor_tensor(res[:, hi], neg[:, hi], -2.0, other_hi[:], ALU.mult, ALU.add)
+            nc.sync.dma_start(out=out[cols(b), hi], in_=res[:, hi])
 
         sc = [scores(b) for b in range(BLOCKS)]
-        abd_picked = gather(abd_t[:], pry_t, F32, "abd_picked")
         grown = grow(0, sc[0])
         for b in range(BLOCKS):
             ahead = grow(b + 1, sc[b + 1]) if b + 1 < BLOCKS else None

from contextlib import ExitStack

import concourse.mybir as mybir

F32 = mybir.dt.float32
BF16 = mybir.dt.bfloat16
I32 = mybir.dt.int32
U32 = mybir.dt.uint32
U16 = mybir.dt.uint16
U8 = mybir.dt.uint8
FP8X4 = mybir.dt.float8_e4m3fn_x4
ACT = mybir.ActivationFunctionType
ALU = mybir.AluOpType

P = 128
PACK = 4
K = 512
N = 512
TABLE = 2048
HALF = N // 2
BLOCKS = N // P
FLOPS = 4 * 2 * K * N * N


def tile_picked_yfoodwb_sw_p_kernel(
    tc, x_words, x_scales, w1, e_words, e_scales, w2, w3, unit, unit2, abd, offs, pry, ref, sw, out
):
    nc = tc.nc
    with ExitStack() as ctx:
        keep = ctx.enter_context(tc.tile_pool(name="keep", bufs=1))
        ring = ctx.enter_context(tc.tile_pool(name="ring", bufs=2))
        psum = ctx.enter_context(tc.psum_pool(name="psum", bufs=1))

        def load_list(src, name):
            t = keep.tile([P, N // 16], U16, name=name)
            nc.sync.dma_start(t[:], src)
            return t

        def load_weight(src, name, tag):
            t = keep.tile([P, PACK, N], F32, name=name, tag=tag, align_bytes=64)
            nc.sync.dma_start(out=t[:], in_=src.rearrange("(p j) c -> p j c", j=PACK))
            return t

        def load_words(src, name, tag):
            t = keep.tile([P, TABLE], I32, name=name, tag=tag, align_bytes=64)
            nc.sync.dma_start(out=t[:], in_=src[0].rearrange("p c r -> p (c r)").bitcast(I32))
            return t

        def load_scale_bytes(src, name, first_row, clear, queue):
            t = keep.tile([P, TABLE], U8, name=name, tag=name, align_bytes=64)
            clear.memset(t[:].bitcast(I32), 0)
            for q in range(4):
                queue.dma_start(
                    out=t[32 * q + first_row : 32 * q + first_row + 4, :].bitcast(I32),
                    in_=src[0, 4 * q : 4 * q + 4, :].bitcast(I32),
                )
            return t

        def load_rows_factor(src, name):
            t = keep.tile([P, PACK], F32, name=name)
            nc.gpsimd.dma_start(out=t[:], in_=src.rearrange("(p t) o -> p (t o)", t=PACK))
            return t

        def gather(table, idx, dtype, name):
            t = keep.tile([P, N], dtype, name=name, align_bytes=64)
            nc.vector.tensor_copy(t[:], table.indirect(idx[:]))
            return t

        def gather_words(table, idx, name):
            t = keep.tile([P, N], U32, name=name, align_bytes=64)
            for h in range(2):
                nc.vector.tensor_copy(t[:, cols(h, HALF)], table[:].bitcast(U32).indirect(idx[:, cols(h, 16)]))
            return t

        def round_weight(raw, name, scalar_share=0):
            g = keep.tile([P, PACK, P, PACK], BF16, name=name, align_bytes=64)
            dst = g[:].rearrange("p t m j -> p m j t")
            src = raw[:].rearrange("p j (m t) -> p m j t", t=PACK)
            if scalar_share:
                nc.scalar.copy(out=dst[:, :scalar_share], in_=src[:, :scalar_share])
            nc.vector.tensor_copy(out=dst[:, scalar_share:], in_=src[:, scalar_share:])
            return g

        def quantize_weight(g, name, tag=None):
            codes = keep.tile([P, N], U32, name=name + "_codes", tag=tag or name, align_bytes=64)
            scales = keep.tile([P, N], U8, name=name + "_scales", align_bytes=64)
            nc.vector.quantize_mx(
                out=codes[:].bitcast(FP8X4), scales=scales[:], in_=g[:].rearrange("p t m j -> p (t m j)")
            )
            return codes, scales

        def product(acc, lhs, lhs_cols, rhs, rhs_cols):
            nc.tensor.matmul_mx(
                out=acc,
                lhsT=lhs[0][:, lhs_cols].bitcast(FP8X4),
                lhsT_scale=lhs[1][:, lhs_cols],
                rhs=rhs[0][:, rhs_cols].bitcast(FP8X4),
                rhs_scale=rhs[1][:, rhs_cols],
                start=True,
                stop=True,
            )

        def cols(b, width=P):
            return slice(b * width, (b + 1) * width)

        E_ROW = 4
        warm = keep.tile([P, 1], F32, name="warm")
        nc.gpsimd.memset(warm[:], 0.0)
        warm_gelu = keep.tile([P, 1], F32, name="warm_gelu")
        nc.scalar.activation(warm_gelu[:], warm[:], ACT.Gelu_apprx_tanh)
        w3_raw = load_weight(w3, "w3_raw", "w3_raw")
        pry_t = load_list(pry, "pry_t")
        e_scale_table = load_scale_bytes(e_scales, "e_scale_table", E_ROW, nc.vector, nc.sync)
        e_table = load_words(e_words, "e_table", "e_table")
        offs_t = load_list(offs, "offs_t")
        x_scale_table = load_scale_bytes(x_scales, "x_scale_table", 0, nc.vector, nc.sync)
        w2_raw = load_weight(w2, "w2_raw", "w2_raw")
        ref_t = load_list(ref, "ref_t")
        w1_raw = load_weight(w1, "w1_raw", "w1_raw")
        x_table = load_words(x_words, "x_table", "x_table")
        sw_t = load_list(sw, "sw_t")
        abd_t = keep.tile([P, TABLE], F32, name="abd_t")
        nc.sync.dma_start(out=abd_t[:], in_=abd)
        unit2_t = load_rows_factor(unit2, "unit2_t")
        unit_t = load_rows_factor(unit, "unit_t")

        e_picked_scales = gather(e_scale_table[:], pry_t, U8, "e_picked_scales")
        w3q = quantize_weight(round_weight(w3_raw, "w3_bf", 80), "w3", "e_scale_table")
        e_picked_words = gather_words(e_table, pry_t, "e_picked_words")
        e_picked = (e_picked_words, e_picked_scales[E_ROW:P, :])
        x_picked_scales = gather(x_scale_table[:], offs_t, U8, "x_picked_scales")

        refuge = keep.tile([P, PACK, N], F32, name="refuge")
        for h in range(2):
            for u in range(2):
                yg = psum.tile([P, 2, HALF], F32, name="yg", tag="a%d" % (2 * h + u))
                for s in range(2):
                    product(yg[:, s, :], w3q, cols(2 * u + s), e_picked, cols(h, HALF))
                nc.scalar.activation(refuge[:, cols(u, 2), cols(h, HALF)], yg[:], ACT.Tanh, scale=0.5)
        w2_bf = round_weight(w2_raw, "w2_bf")
        w2q = quantize_weight(w2_bf, "w2")

        fetched = [keep.tile([P, PACK, HALF], F32, name="fetched%d" % h) for h in range(2)]
        for h in range(2):
            for t in range(PACK):
                piece = fetched[h][:, t, :]
                nc.scalar.activation(
                    piece, refuge[:, t, :].indirect(ref_t[:, cols(h, 16)]), ACT.Copy, scale=-0.35, bias=0.85
                )
                nc.gpsimd.tensor_scalar(piece, piece, unit2_t[:, t : t + 1], 0.0, ALU.mult, ALU.add)

        ye = []
        for b in range(BLOCKS):
            bank = psum.tile([P, PACK, P], F32, name="ye", tag="b%d" % b)
            for t in range(PACK):
                product(bank[:, t, :], w2q, cols(t), e_picked, cols(b))
            ye.append(bank)

        w1q = quantize_weight(round_weight(w1_raw, "w1_bf"), "w1")
        x_picked_words = gather_words(x_table, offs_t, "x_picked_words")
        x_picked = (x_picked_words, x_picked_scales)

        att = []
        for b in range(BLOCKS):
            bank = psum.tile([P, PACK, P], F32, name="y", tag="a%d" % b)
            for t in range(PACK):
                product(bank[:, t, :], w1q, cols(t), x_picked, cols(b))
            a = keep.tile([P, P, PACK], F32, name="att%d" % b)
            nc.scalar.activation(a[:], bank[:].rearrange("p t j -> p j t"), ACT.Gelu_apprx_tanh)
            att.append(a)

        WIDE = N + 1
        abd_picked = keep.tile([P, WIDE], F32, name="abd_picked")
        nc.gpsimd.memset(abd_picked[:, N:WIDE], N / 2.0)
        nc.scalar.activation(abd_picked[:, :N], abd_t[:].indirect(pry_t[:]), ACT.Copy)
        warm_exp = keep.tile([P, 1], F32, name="warm_exp")
        nc.scalar.activation(warm_exp[:], att[BLOCKS - 1][:, 0, 0:1], ACT.Exp, scale=0.0)
        hid2_bf = keep.tile([P, N, PACK], BF16, name="hid2_bf", tag="x_table", align_bytes=64)
        for b in range(BLOCKS):
            nc.vector.tensor_tensor(
                hid2_bf[:, cols(b), :].rearrange("p (c i) t -> p c t i", i=4),
                ye[b][:].rearrange("p t (c i) -> p c t i", i=4),
                fetched[b // 2][:, :, cols(b % 2)].rearrange("p t (c i) -> p c t i", i=4),
                ALU.mult,
            )
        hid2_codes = keep.tile([P, N], U32, name="hid2_codes", align_bytes=64)
        hid2_scales = keep.tile([P, N], U8, name="hid2_scales", align_bytes=64)
        for h in range(2):
            nc.vector.quantize_mx(
                out=hid2_codes[:, cols(h, HALF)].bitcast(FP8X4),
                scales=hid2_scales[:, cols(h, HALF)],
                in_=hid2_bf[:, cols(h, HALF), :].rearrange("p e t -> p (e t)"),
            )


        def scores(b):
            hid_bf = keep.tile([P, P, PACK], BF16, name="hid_bf%d" % b, align_bytes=64)
            nc.vector.tensor_tensor(
                hid_bf[:], att[b][:], unit_t[:].unsqueeze(1).to_broadcast([P, P, PACK]), ALU.mult
            )
            codes = keep.tile([P, P], U32, name="hid_codes%d" % b, align_bytes=64)
            scales = keep.tile([P, P], U8, name="hid_scales%d" % b, align_bytes=64)
            nc.vector.quantize_mx(
                out=codes[:].bitcast(FP8X4), scales=scales[:], in_=hid_bf[:].rearrange("p j t -> p (j t)")
            )
            sc = psum.tile([P, N], F32, name="sc", tag="b%d" % b)
            product(sc[:], (codes, scales), slice(0, P), (hid2_codes, hid2_scales), slice(0, N))
            return sc

        def grow(b, sc):
            bounded = ring.tile([P, N], F32, name="bounded")
            nc.scalar.activation(bounded[:], sc[:], ACT.Tanh)
            grown = keep.tile([P, WIDE], F32, name="grown%d" % b)
            nc.gpsimd.memset(grown[:, N:WIDE], 1.0)
            nc.scalar.activation(grown[:, :N], bounded[:], ACT.Exp, scale=1.2)
            return grown

        def finish(b, grown):
            rate = keep.tile([P, WIDE], F32, name="rate%d" % b)
            total = keep.tile([P, 1], F32, name="total%d" % b)
            nc.vector.scalar_tensor_tensor(
                rate[:], grown[:], 1.0, abd_picked[:], ALU.mult, ALU.mult, accum_out=total[:]
            )
            inv = keep.tile([P, 1], F32, name="inv%d" % b)
            nc.vector.reciprocal(inv[:], total[:])
            res = keep.tile([P, N], F32, name="res%d" % b)
            if b < BLOCKS - 2:
                feed = keep.tile([P, WIDE], F32, name="feed%d" % b)
                nc.vector.tensor_scalar(feed[:], rate[:], inv[:], float(N), ALU.mult, ALU.mult)
                other = keep.tile([P, N], F32, name="other%d" % b)
                nc.scalar.activation(other[:], feed[:].indirect(sw_t[:]), ACT.Copy, scale=-0.5)
                nc.vector.tensor_tensor(res[:], feed[:, :N], other[:], ALU.add)
                nc.sync.dma_start(out=out[cols(b), :], in_=res[:])
                return
            lo, hi = cols(0, HALF), cols(1, HALF)
            neg = keep.tile([P, N], F32, name="neg%d" % b)
            nc.vector.tensor_scalar(neg[:], rate[:, :N], inv[:], -0.5 * N, ALU.mult, ALU.mult)
            feed_lo = keep.tile([P, HALF], F32, name="feed_lo%d" % b)
            nc.vector.tensor_scalar(feed_lo[:], rate[:, lo], inv[:], float(N), ALU.mult, ALU.mult)
            other_hi = keep.tile([P, HALF], F32, name="other_hi%d" % b)
            nc.scalar.activation(other_hi[:], neg[:].indirect(sw_t[:, cols(1, 16)]), ACT.Copy)
            nc.vector.tensor_tensor(res[:, lo], neg[:].indirect(sw_t[:, cols(0, 16)]), feed_lo[:], ALU.add)
            nc.sync.dma_start(out=out[cols(b), lo], in_=res[:, lo])
            nc.vector.scalar_tensor_tensor(res[:, hi], neg[:, hi], -2.0, other_hi[:], ALU.mult, ALU.add)
            nc.sync.dma_start(out=out[cols(b), hi], in_=res[:, hi])

        sc = [scores(b) for b in range(BLOCKS)]
        grown = grow(0, sc[0])
        for b in range(BLOCKS):
            ahead = grow(b + 1, sc[b + 1]) if b + 1 < BLOCKS else None
            finish(b, grown)
            grown = ahead
